import numpy as np
import ml_dtypes


def mxq(x, axis, fmt="e4m3"):
    dtype, down = {"e4m3": (ml_dtypes.float8_e4m3fn, 7), "e5m2": (ml_dtypes.float8_e5m2, 14)}[fmt]
    v = np.moveaxis(np.asarray(x, np.float32).astype(ml_dtypes.bfloat16).astype(np.float64), axis, -1)
    blocks = v.reshape(v.shape[:-1] + (-1, 32))
    amax = np.abs(blocks).max(-1, keepdims=True)
    byte = np.maximum(np.where(amax > 0, np.frexp(amax)[1] - 1 + 127, 0) - down, 1)
    scale = np.exp2(byte - 127.0)
    codes = (blocks / scale).astype(np.float32).astype(dtype).astype(np.float64)
    return np.moveaxis((codes * scale).reshape(v.shape), -1, axis)


WIDE = False


def mx_kscale(k):
    if not WIDE:
        return np.ones(k)
    levels = np.array([10, -10, 5, -5, 0])
    if k % 512:
        return np.exp2(np.random.permutation(np.resize(levels, k // 32))).repeat(32)
    a = np.empty((k // 512, 16))
    for p in range(k // 512):
        a[p, :8] = np.random.permutation(np.resize(levels, 8))
        for g in range(8):
            far = levels[np.abs(levels - a[p, g]) >= 10]
            a[p, g + 8] = far[np.random.randint(len(far))]
    return np.exp2(a.ravel()).repeat(32)


def f64(x):
    return np.asarray(x).astype(np.float64)


def striped(idx):
    return np.tile(idx.reshape(-1, 16).T, (8, 1)).astype(np.uint16)


def unstriped(offs):
    return offs[:16].T.reshape(-1).astype(np.int64)


def pack_weight(w):
    k, n = w.shape
    w = f64(np.asarray(w, np.float32).astype(ml_dtypes.bfloat16)).reshape(k // 32, 32, n)
    amax = np.abs(w).max(1)
    byte = np.clip(np.where(amax > 0, np.frexp(amax)[1] - 1 + 127 - 7, 1), 1, 254)
    scaled = (w * np.exp2(127.0 - byte)[:, None, :]).reshape(k, n).astype(np.float32)
    words = np.ascontiguousarray(scaled.reshape(k // 512, 128, 4, n).transpose(0, 1, 3, 2)).astype(ml_dtypes.float8_e4m3fn).view(np.uint8)
    return words, np.ascontiguousarray(byte.astype(np.uint8).reshape(k // 512, 16, n))


def unpack_weight(words, scales):
    g, p, n, _ = words.shape
    vals = np.ascontiguousarray(words).view(ml_dtypes.float8_e4m3fn).astype(np.float64) * np.repeat(np.exp2(scales.astype(np.float64) - 127.0), 8, axis=1)[..., None]
    return vals.transpose(0, 1, 3, 2).reshape(g * 512, n)


K, T, S, N = 512, 1024, 512, 256
P = 2 ** 7


def setup_inputs():
    n = np.random.standard_normal
    s = mx_kscale(K)[:, None]
    packed_w1 = pack_weight(n((K, N)) / np.sqrt(K) / s)
    return {
        "xT": (n((K, T)) * s).astype(np.float32),
        "w1_words": packed_w1[0],
        "w1_scales": packed_w1[1],
        "prior": np.tile(0.5 * np.random.standard_normal(S), (P, 1)).astype(np.float32),
        "offs": striped(np.random.permutation(T)[:S]),
    }


def reference(xT, w1_words, w1_scales, prior, offs):
    xq = mxq(f64(xT)[:, unstriped(offs)], 0, "e4m3")
    y = unpack_weight(w1_words, w1_scales).T @ xq
    yp = y + f64(prior)[:1]
    e = np.exp(yp - yp.max(axis=1, keepdims=True))
    return e / e.sum(axis=1, keepdims=True)

@@ -1,0 +1,105 @@
+from contextlib import ExitStack
+
+import concourse.mybir as mybir
+
+K, T, S, N = 512, 1024, 512, 256
+P = 128
+FLOPS = 2 * K * S * N
+
+F32 = mybir.dt.float32
+BF16 = mybir.dt.bfloat16
+I32 = mybir.dt.int32
+U32 = mybir.dt.uint32
+U16 = mybir.dt.uint16
+U8 = mybir.dt.uint8
+FP8X4 = mybir.dt.float8_e4m3fn_x4
+ALU = mybir.AluOpType
+ACT = mybir.ActivationFunctionType
+
+CHUNKS = (
+    ((0, 512, 0), (512, 1024, 352)),
+    ((0, 512, 0), (512, 768, 256), (768, 1024, 176)),
+)
+Q = 128
+H = 256
+
+
+def tile_picked_rank_prior_e_kernel(tc, xT, w1_words, w1_scales, prior, offs, out):
+    nc = tc.nc
+    x4 = xT.rearrange("(p j) t -> p j t", j=4)
+    with ExitStack() as ctx:
+        keep = ctx.enter_context(tc.tile_pool(name="keep", bufs=1))
+        psum = ctx.enter_context(tc.psum_pool(name="psum", bufs=1))
+
+        offsets = keep.tile([P, S // 16], U16, name="offsets")
+        w_codes = keep.tile([P, N], U32, name="w_codes", align_bytes=64)
+        w_scales = keep.tile([P, N], U8, name="w_scales", align_bytes=64)
+        prior_sb = keep.tile([P, S], F32, name="prior_sb")
+        nc.gpsimd.memset(w_scales[:].bitcast(I32), 0)
+
+        raw = {}
+        for u in range(2):
+            for c, (c0, c1, cv) in enumerate(CHUNKS[u]):
+                t = keep.tile([P, 2, c1 - c0], F32, name="raw%d_%d" % (u, c))
+                nc.sync.dma_start(out=t[:], in_=x4[:, 2 * u : 2 * u + 2, c0:c1])
+                raw[u, c] = t
+                if (u, c) == (0, 0):
+                    nc.sync.dma_start(offsets[:], offs)
+        nc.sync.dma_start(out=w_codes[:].bitcast(I32), in_=w1_words[0].rearrange("p n t -> p (n t)").bitcast(I32))
+        for q in range(4):
+            nc.sync.dma_start(out=w_scales[32 * q : 32 * q + 4, :].bitcast(I32), in_=w1_scales[0, 4 * q : 4 * q + 4, :].bitcast(I32))
+        nc.sync.dma_start(out=prior_sb[:], in_=prior)
+
+        windows = [keep.tile([P, 2 * T], BF16, name="window%d" % u, align_bytes=64) for u in range(2)]
+        picked = [keep.tile([P, 2, Q], U32, name="picked%d" % i, align_bytes=64) for i in range(S // Q)]
+
+        def cast(u, c):
+            c0, c1, cv = CHUNKS[u][c]
+            src = raw[u, c][:].rearrange("p e t -> p t e")
+            dst = windows[u][:, 2 * c0 : 2 * c1].rearrange("p (t e) -> p t e", e=2)
+            if cv < c1 - c0:
+                nc.scalar.activation(out=dst[:, cv:, :], in_=src[:, cv:, :], func=ACT.Copy)
+            if cv > 0:
+                nc.vector.tensor_copy(out=dst[:, :cv, :], in_=src[:, :cv, :])
+
+        def gather(u, i):
+            nc.vector.tensor_copy(picked[i][:, u, :], windows[u][:].bitcast(U32).indirect(offsets[:, i * Q // 16 : (i + 1) * Q // 16]))
+
+        for c in range(len(CHUNKS[0])):
+            cast(0, c)
+        for i in range(S // Q):
+            gather(0, i)
+        for c in range(len(CHUNKS[1])):
+            cast(1, c)
+
+        grouped = [keep.tile([P, 4 * Q], BF16, name="grouped%d" % i, align_bytes=64) for i in range(S // Q)]
+        x_codes = [keep.tile([P, H], U32, name="x_codes%d" % h, align_bytes=64) for h in range(2)]
+        x_scales = [keep.tile([P, H], U8, name="x_scales%d" % h, align_bytes=64) for h in range(2)]
+        for i in range(S // Q):
+            gather(1, i)
+            nc.scalar.copy(out=grouped[i][:].bitcast(U32).rearrange("p (n u) -> p n u", u=2), in_=picked[i][:].rearrange("p u n -> p n u"))
+        scores = {(m, h): psum.tile([P, H], F32, name="scores%d_%d" % (m, h)) for m in range(2) for h in range(2)}
+        for i in range(S // Q):
+            h, r = divmod(i, 2)
+            cols = slice(r * Q, (r + 1) * Q)
+            nc.vector.quantize_mx(out=x_codes[h][:, cols].bitcast(FP8X4), scales=x_scales[h][:, cols], in_=grouped[i][:])
+            for m in range(2):
+                nc.tensor.matmul_mx(out=scores[m, h][:, cols], lhsT=w_codes[:, m * P : (m + 1) * P].bitcast(FP8X4), lhsT_scale=w_scales[:, m * P : (m + 1) * P],
+                                    rhs=x_codes[h][:, cols].bitcast(FP8X4), rhs_scale=x_scales[h][:, cols], start=True, stop=True)
+
+        neg = [keep.tile([P, S], F32, name="neg%d" % m) for m in range(2)]
+        for h in range(2):
+            for m in range(2):
+                nc.vector.scalar_tensor_tensor(out=neg[m][:, h * H : (h + 1) * H], in0=scores[m, h][:], scalar=-1.0, in1=prior_sb[:, h * H : (h + 1) * H], op0=ALU.mult, op1=ALU.subtract)
+        low = [keep.tile([P, 1], F32, name="low%d" % m) for m in range(2)]
+        total = [keep.tile([P, 1], F32, name="total%d" % m) for m in range(2)]
+        inv = [keep.tile([P, 1], F32, name="inv%d" % m) for m in range(2)]
+        ex = [keep.tile([P, S], F32, name="ex%d" % m) for m in range(2)]
+        res = [keep.tile([P, S], F32, name="res%d" % m) for m in range(2)]
+        for m in range(2):
+            nc.vector.tensor_reduce(out=low[m][:], in_=neg[m][:], axis=mybir.AxisListType.X, op=ALU.min)
+            nc.scalar.activation(out=ex[m][:], in_=neg[m][:], func=ACT.Exp, bias=low[m][:], scale=-1.0, accum_out=total[m][:])
+        for m in range(2):
+            nc.vector.reciprocal(out=inv[m][:], in_=total[m][:])
+            nc.vector.tensor_scalar(out=res[m][:], in0=ex[m][:], scalar1=inv[m][:], scalar2=None, op0=ALU.mult)
+            nc.sync.dma_start(out=out[m * P : (m + 1) * P, :], in_=res[m][:])

@@ -17,8 +17,8 @@ ALU = mybir.AluOpType
 ACT = mybir.ActivationFunctionType
 
 CHUNKS = (
-    ((0, 512, 0), (512, 1024, 352)),
-    ((0, 512, 0), (512, 768, 256), (768, 1024, 176)),
+    ((0, 768, 512), (768, 1024, 176)),
+    ((0, 384, 0), (384, 768, 256), (768, 1024, 176)),
 )
 Q = 128
 H = 256
@@ -35,7 +35,7 @@ def tile_picked_rank_prior_e_kernel(tc, xT, w1_words, w1_scales, prior, offs, ou
         w_codes = keep.tile([P, N], U32, name="w_codes", align_bytes=64)
         w_scales = keep.tile([P, N], U8, name="w_scales", align_bytes=64)
         prior_sb = keep.tile([P, S], F32, name="prior_sb")
-        nc.gpsimd.memset(w_scales[:].bitcast(I32), 0)
+        nc.vector.memset(w_scales[:].bitcast(I32), 0)
 
         raw = {}
         for u in range(2):
@@ -51,7 +51,7 @@ def tile_picked_rank_prior_e_kernel(tc, xT, w1_words, w1_scales, prior, offs, ou
         nc.sync.dma_start(out=prior_sb[:], in_=prior)
 
         windows = [keep.tile([P, 2 * T], BF16, name="window%d" % u, align_bytes=64) for u in range(2)]
-        picked = [keep.tile([P, 2, Q], U32, name="picked%d" % i, align_bytes=64) for i in range(S // Q)]
+        picked = keep.tile([P, 2, S], U32, name="picked", tag="picked", align_bytes=64)
 
         def cast(u, c):
             c0, c1, cv = CHUNKS[u][c]
@@ -62,32 +62,40 @@ def tile_picked_rank_prior_e_kernel(tc, xT, w1_words, w1_scales, prior, offs, ou
             if cv > 0:
                 nc.vector.tensor_copy(out=dst[:, :cv, :], in_=src[:, :cv, :])
 
-        def gather(u, i):
-            nc.vector.tensor_copy(picked[i][:, u, :], windows[u][:].bitcast(U32).indirect(offsets[:, i * Q // 16 : (i + 1) * Q // 16]))
+        def gather(u, dst, first, count):
+            nc.vector.tensor_copy(dst, windows[u][:].bitcast(U32).indirect(offsets[:, first // 16 : (first + count) // 16]))
 
         for c in range(len(CHUNKS[0])):
             cast(0, c)
-        for i in range(S // Q):
-            gather(0, i)
+        gather(0, picked[:, 0, :], 0, S)
         for c in range(len(CHUNKS[1])):
             cast(1, c)
 
+        both = [picked[:, :, i * Q : (i + 1) * Q] for i in range(S // Q)]
         grouped = [keep.tile([P, 4 * Q], BF16, name="grouped%d" % i, align_bytes=64) for i in range(S // Q)]
         x_codes = [keep.tile([P, H], U32, name="x_codes%d" % h, align_bytes=64) for h in range(2)]
         x_scales = [keep.tile([P, H], U8, name="x_scales%d" % h, align_bytes=64) for h in range(2)]
-        for i in range(S // Q):
-            gather(1, i)
-            nc.scalar.copy(out=grouped[i][:].bitcast(U32).rearrange("p (n u) -> p n u", u=2), in_=picked[i][:].rearrange("p u n -> p n u"))
         scores = {(m, h): psum.tile([P, H], F32, name="scores%d_%d" % (m, h)) for m in range(2) for h in range(2)}
-        for i in range(S // Q):
+
+        def pick(i):
+            gather(1, both[i][:, 1, :], i * Q, Q)
+            nc.scalar.copy(out=grouped[i][:].bitcast(U32).rearrange("p (n u) -> p n u", u=2), in_=both[i].rearrange("p u n -> p n u"))
+
+        def score(i):
             h, r = divmod(i, 2)
             cols = slice(r * Q, (r + 1) * Q)
             nc.vector.quantize_mx(out=x_codes[h][:, cols].bitcast(FP8X4), scales=x_scales[h][:, cols], in_=grouped[i][:])
-            for m in range(2):
-                nc.tensor.matmul_mx(out=scores[m, h][:, cols], lhsT=w_codes[:, m * P : (m + 1) * P].bitcast(FP8X4), lhsT_scale=w_scales[:, m * P : (m + 1) * P],
-                                    rhs=x_codes[h][:, cols].bitcast(FP8X4), rhs_scale=x_scales[h][:, cols], start=True, stop=True)
+            for m, use in ((0, cols), (1, slice(0, H)))[: r + 1]:
+                nc.tensor.matmul_mx(out=scores[m, h][:, use], lhsT=w_codes[:, m * P : (m + 1) * P].bitcast(FP8X4), lhsT_scale=w_scales[:, m * P : (m + 1) * P],
+                                    rhs=x_codes[h][:, use].bitcast(FP8X4), rhs_scale=x_scales[h][:, use], start=True, stop=True)
 
-        neg = [keep.tile([P, S], F32, name="neg%d" % m) for m in range(2)]
+        for i in range(4):
+            pick(i)
+        for i in range(4):
+            score(i)
+
+        neg_all = keep.tile([P, 2 * S], F32, name="neg_all", tag="picked", align_bytes=64)
+        neg = [neg_all[:, m * S : (m + 1) * S] for m in range(2)]
         for h in range(2):
             for m in range(2):
                 nc.vector.scalar_tensor_tensor(out=neg[m][:, h * H : (h + 1) * H], in0=scores[m, h][:], scalar=-1.0, in1=prior_sb[:, h * H : (h + 1) * H], op0=ALU.mult, op1=ALU.subtract)
@@ -97,9 +105,10 @@ def tile_picked_rank_prior_e_kernel(tc, xT, w1_words, w1_scales, prior, offs, ou
         ex = [keep.tile([P, S], F32, name="ex%d" % m) for m in range(2)]
         res = [keep.tile([P, S], F32, name="res%d" % m) for m in range(2)]
         for m in range(2):
-            nc.vector.tensor_reduce(out=low[m][:], in_=neg[m][:], axis=mybir.AxisListType.X, op=ALU.min)
-            nc.scalar.activation(out=ex[m][:], in_=neg[m][:], func=ACT.Exp, bias=low[m][:], scale=-1.0, accum_out=total[m][:])
+            nc.vector.tensor_reduce(out=low[m][:], in_=neg[m], axis=mybir.AxisListType.X, op=ALU.min)
+            nc.scalar.activation(out=ex[m][:], in_=neg[m], func=ACT.Exp, bias=low[m][:], scale=-1.0, accum_out=total[m][:])
         for m in range(2):
             nc.vector.reciprocal(out=inv[m][:], in_=total[m][:])
-            nc.vector.tensor_scalar(out=res[m][:], in0=ex[m][:], scalar1=inv[m][:], scalar2=None, op0=ALU.mult)
-            nc.sync.dma_start(out=out[m * P : (m + 1) * P, :], in_=res[m][:])
+            for cols in ([slice(0, S)], [slice(0, H), slice(H, S)])[m]:
+                nc.vector.tensor_scalar(out=res[m][:, cols], in0=ex[m][:, cols], scalar1=inv[m][:], scalar2=None, op0=ALU.mult)
+                nc.sync.dma_start(out=out[m * P : (m + 1) * P, cols], in_=res[m][:, cols])

@@ -16,10 +16,6 @@ FP8X4 = mybir.dt.float8_e4m3fn_x4
 ALU = mybir.AluOpType
 ACT = mybir.ActivationFunctionType
 
-CHUNKS = (
-    ((0, 768, 512), (768, 1024, 176)),
-    ((0, 384, 0), (384, 768, 256), (768, 1024, 176)),
-)
 Q = 128
 H = 256
 
@@ -37,64 +33,61 @@ def tile_picked_rank_prior_e_kernel(tc, xT, w1_words, w1_scales, prior, offs, ou
         prior_sb = keep.tile([P, S], F32, name="prior_sb")
         nc.vector.memset(w_scales[:].bitcast(I32), 0)
 
-        raw = {}
-        for u in range(2):
-            for c, (c0, c1, cv) in enumerate(CHUNKS[u]):
-                t = keep.tile([P, 2, c1 - c0], F32, name="raw%d_%d" % (u, c))
-                nc.sync.dma_start(out=t[:], in_=x4[:, 2 * u : 2 * u + 2, c0:c1])
-                raw[u, c] = t
-                if (u, c) == (0, 0):
-                    nc.sync.dma_start(offsets[:], offs)
+        warm_in = keep.tile([P, 1], F32, name="warm_in")
+        warm_out = keep.tile([P, 1], F32, name="warm_out")
+        nc.vector.memset(warm_in[:], 0.0)
+        nc.scalar.activation(out=warm_out[:], in_=warm_in[:], func=ACT.Exp)
+
+        planes = [keep.tile([P, T], F32, name="plane%d" % j, align_bytes=64) for j in range(4)]
+        for j in range(4):
+            nc.sync.dma_start(out=planes[j][:], in_=x4[:, j, :])
+            if j == 0:
+                nc.sync.dma_start(offsets[:], offs)
         nc.sync.dma_start(out=w_codes[:].bitcast(I32), in_=w1_words[0].rearrange("p n t -> p (n t)").bitcast(I32))
         for q in range(4):
             nc.sync.dma_start(out=w_scales[32 * q : 32 * q + 4, :].bitcast(I32), in_=w1_scales[0, 4 * q : 4 * q + 4, :].bitcast(I32))
         nc.sync.dma_start(out=prior_sb[:], in_=prior)
 
-        windows = [keep.tile([P, 2 * T], BF16, name="window%d" % u, align_bytes=64) for u in range(2)]
-        picked = keep.tile([P, 2, S], U32, name="picked", tag="picked", align_bytes=64)
+        def window(j, first, count):
+            return planes[j][:].indirect(offsets[:, first // 16 : (first + count) // 16])
 
-        def cast(u, c):
-            c0, c1, cv = CHUNKS[u][c]
-            src = raw[u, c][:].rearrange("p e t -> p t e")
-            dst = windows[u][:, 2 * c0 : 2 * c1].rearrange("p (t e) -> p t e", e=2)
-            if cv < c1 - c0:
-                nc.scalar.activation(out=dst[:, cv:, :], in_=src[:, cv:, :], func=ACT.Copy)
-            if cv > 0:
-                nc.vector.tensor_copy(out=dst[:, :cv, :], in_=src[:, :cv, :])
+        grouped = [keep.tile([P, Q, 4], BF16, name="grouped%d" % i, align_bytes=64) for i in range(4)]
+        low_pair = [keep.tile([P, 2, H], BF16, name="low_pair%d" % h, align_bytes=64) for h in range(2)]
+        high_pair = keep.tile([P, 2, 1024], BF16, name="high_pair", tag="high", align_bytes=64)
 
-        def gather(u, dst, first, count):
-            nc.vector.tensor_copy(dst, windows[u][:].bitcast(U32).indirect(offsets[:, first // 16 : (first + count) // 16]))
+        for j in range(2):
+            nc.vector.tensor_copy(low_pair[0][:, j, :], window(j, 0, H))
+            nc.scalar.activation(out=low_pair[1][:, j, :], in_=window(j, H, H), func=ACT.Copy)
+        for i in range(4):
+            h, r = divmod(i, 2)
+            nc.vector.tensor_copy(out=grouped[i][:, :, 0:2], in_=low_pair[h][:, :, r * Q : (r + 1) * Q].rearrange("p e n -> p n e"))
+        nc.vector.tensor_copy(grouped[0][:, :, 2], window(2, 0, Q))
+        nc.scalar.activation(out=high_pair[:, 0, Q:S], in_=window(2, Q, S - Q), func=ACT.Copy)
 
-        for c in range(len(CHUNKS[0])):
-            cast(0, c)
-        gather(0, picked[:, 0, :], 0, S)
-        for c in range(len(CHUNKS[1])):
-            cast(1, c)
-
-        both = [picked[:, :, i * Q : (i + 1) * Q] for i in range(S // Q)]
-        grouped = [keep.tile([P, 4 * Q], BF16, name="grouped%d" % i, align_bytes=64) for i in range(S // Q)]
         x_codes = [keep.tile([P, H], U32, name="x_codes%d" % h, align_bytes=64) for h in range(2)]
         x_scales = [keep.tile([P, H], U8, name="x_scales%d" % h, align_bytes=64) for h in range(2)]
         scores = {(m, h): psum.tile([P, H], F32, name="scores%d_%d" % (m, h)) for m in range(2) for h in range(2)}
 
-        def pick(i):
-            gather(1, both[i][:, 1, :], i * Q, Q)
-            nc.scalar.copy(out=grouped[i][:].bitcast(U32).rearrange("p (n u) -> p n u", u=2), in_=both[i].rearrange("p u n -> p n u"))
+        def insert(i):
+            nc.vector.tensor_copy(out=grouped[i][:, :, 2:4], in_=high_pair[:, :, i * Q : (i + 1) * Q].rearrange("p e n -> p n e"))
 
         def score(i):
             h, r = divmod(i, 2)
             cols = slice(r * Q, (r + 1) * Q)
-            nc.vector.quantize_mx(out=x_codes[h][:, cols].bitcast(FP8X4), scales=x_scales[h][:, cols], in_=grouped[i][:])
+            nc.vector.quantize_mx(out=x_codes[h][:, cols].bitcast(FP8X4), scales=x_scales[h][:, cols], in_=grouped[i][:].rearrange("p n t -> p (n t)"))
             for m, use in ((0, cols), (1, slice(0, H)))[: r + 1]:
                 nc.tensor.matmul_mx(out=scores[m, h][:, use], lhsT=w_codes[:, m * P : (m + 1) * P].bitcast(FP8X4), lhsT_scale=w_scales[:, m * P : (m + 1) * P],
                                     rhs=x_codes[h][:, use].bitcast(FP8X4), rhs_scale=x_scales[h][:, use], start=True, stop=True)
 
-        for i in range(4):
-            pick(i)
-        for i in range(4):
-            score(i)
+        nc.vector.tensor_copy(grouped[0][:, :, 3], window(3, 0, Q))
+        for i in range(1, 4):
+            nc.scalar.activation(out=high_pair[:, 1, i * Q : (i + 1) * Q], in_=window(3, i * Q, Q), func=ACT.Copy)
+        for i in range(1, 4):
+            insert(i)
+            score(i - 1)
+        score(3)
 
-        neg_all = keep.tile([P, 2 * S], F32, name="neg_all", tag="picked", align_bytes=64)
+        neg_all = keep.tile([P, 2 * S], F32, name="neg_all", tag="high", align_bytes=64)
         neg = [neg_all[:, m * S : (m + 1) * S] for m in range(2)]
         for h in range(2):
             for m in range(2):

@@ -30,7 +30,7 @@ def tile_picked_rank_prior_e_kernel(tc, xT, w1_words, w1_scales, prior, offs, ou
         offsets = keep.tile([P, S // 16], U16, name="offsets")
         w_codes = keep.tile([P, N], U32, name="w_codes", align_bytes=64)
         w_scales = keep.tile([P, N], U8, name="w_scales", align_bytes=64)
-        prior_sb = keep.tile([P, S], F32, name="prior_sb")
+        prior_sb = keep.tile([P, S], F32, name="prior_sb", tag="prior")
         nc.vector.memset(w_scales[:].bitcast(I32), 0)
 
         warm_in = keep.tile([P, 1], F32, name="warm_in")
@@ -52,47 +52,52 @@ def tile_picked_rank_prior_e_kernel(tc, xT, w1_words, w1_scales, prior, offs, ou
             return planes[j][:].indirect(offsets[:, first // 16 : (first + count) // 16])
 
         grouped = [keep.tile([P, Q, 4], BF16, name="grouped%d" % i, align_bytes=64) for i in range(4)]
-        low_pair = [keep.tile([P, 2, H], BF16, name="low_pair%d" % h, align_bytes=64) for h in range(2)]
-        high_pair = keep.tile([P, 2, 1024], BF16, name="high_pair", tag="high", align_bytes=64)
+        low_pair = keep.tile([P, 2, H], BF16, name="low_pair", align_bytes=64)
+        high_pair = keep.tile([P, 2, H], BF16, name="high_pair", tag="high", align_bytes=64)
 
-        for j in range(2):
-            nc.vector.tensor_copy(low_pair[0][:, j, :], window(j, 0, H))
-            nc.scalar.activation(out=low_pair[1][:, j, :], in_=window(j, H, H), func=ACT.Copy)
-        for i in range(4):
-            h, r = divmod(i, 2)
-            nc.vector.tensor_copy(out=grouped[i][:, :, 0:2], in_=low_pair[h][:, :, r * Q : (r + 1) * Q].rearrange("p e n -> p n e"))
-        nc.vector.tensor_copy(grouped[0][:, :, 2], window(2, 0, Q))
-        nc.scalar.activation(out=high_pair[:, 0, Q:S], in_=window(2, Q, S - Q), func=ACT.Copy)
+        def pair_view(pair, r):
+            return pair[:, :, r * Q : (r + 1) * Q].rearrange("p e n -> p n e")
 
-        x_codes = [keep.tile([P, H], U32, name="x_codes%d" % h, align_bytes=64) for h in range(2)]
-        x_scales = [keep.tile([P, H], U8, name="x_scales%d" % h, align_bytes=64) for h in range(2)]
-        scores = {(m, h): psum.tile([P, H], F32, name="scores%d_%d" % (m, h)) for m in range(2) for h in range(2)}
+        for j in range(3):
+            for i in range(2):
+                nc.vector.tensor_copy(grouped[i][:, :, j], window(j, i * Q, Q))
+            nc.scalar.activation(out=(low_pair, high_pair)[j // 2][:, j % 2, :], in_=window(j, H, H), func=ACT.Copy)
+            if j == 1:
+                for r in range(2):
+                    nc.vector.tensor_copy(out=grouped[2 + r][:, :, 0:2], in_=pair_view(low_pair, r))
 
-        def insert(i):
-            nc.vector.tensor_copy(out=grouped[i][:, :, 2:4], in_=high_pair[:, :, i * Q : (i + 1) * Q].rearrange("p e n -> p n e"))
+        x_codes = [keep.tile([P, Q], U32, name="x_codes%d" % i, align_bytes=64) for i in range(4)]
+        x_scales = [keep.tile([P, Q], U8, name="x_scales%d" % i, align_bytes=64) for i in range(4)]
+        early = [psum.tile([P, 2, Q], F32, name="early%d" % i) for i in range(2)]
+        late0 = [psum.tile([P, Q], F32, name="late0_%d" % r) for r in range(2)]
+        late1 = psum.tile([P, H], F32, name="late1")
 
         def score(i):
-            h, r = divmod(i, 2)
-            cols = slice(r * Q, (r + 1) * Q)
-            nc.vector.quantize_mx(out=x_codes[h][:, cols].bitcast(FP8X4), scales=x_scales[h][:, cols], in_=grouped[i][:].rearrange("p n t -> p (n t)"))
-            for m, use in ((0, cols), (1, slice(0, H)))[: r + 1]:
-                nc.tensor.matmul_mx(out=scores[m, h][:, use], lhsT=w_codes[:, m * P : (m + 1) * P].bitcast(FP8X4), lhsT_scale=w_scales[:, m * P : (m + 1) * P],
-                                    rhs=x_codes[h][:, use].bitcast(FP8X4), rhs_scale=x_scales[h][:, use], start=True, stop=True)
-
-        nc.vector.tensor_copy(grouped[0][:, :, 3], window(3, 0, Q))
-        for i in range(1, 4):
-            nc.scalar.activation(out=high_pair[:, 1, i * Q : (i + 1) * Q], in_=window(3, i * Q, Q), func=ACT.Copy)
-        for i in range(1, 4):
-            insert(i)
-            score(i - 1)
-        score(3)
-
-        neg_all = keep.tile([P, 2 * S], F32, name="neg_all", tag="high", align_bytes=64)
-        neg = [neg_all[:, m * S : (m + 1) * S] for m in range(2)]
-        for h in range(2):
+            nc.vector.quantize_mx(out=x_codes[i][:].bitcast(FP8X4), scales=x_scales[i][:], in_=grouped[i][:].rearrange("p n t -> p (n t)"))
             for m in range(2):
-                nc.vector.scalar_tensor_tensor(out=neg[m][:, h * H : (h + 1) * H], in0=scores[m, h][:], scalar=-1.0, in1=prior_sb[:, h * H : (h + 1) * H], op0=ALU.mult, op1=ALU.subtract)
-        low = [keep.tile([P, 1], F32, name="low%d" % m) for m in range(2)]
+                bank = early[i][:, m, :] if i < 2 else (late0[i - 2][:], late1[:, (i - 2) * Q : (i - 1) * Q])[m]
+                nc.tensor.matmul_mx(out=bank, lhsT=w_codes[:, m * P : (m + 1) * P].bitcast(FP8X4), lhsT_scale=w_scales[:, m * P : (m + 1) * P],
+                                    rhs=x_codes[i][:].bitcast(FP8X4), rhs_scale=x_scales[i][:], start=True, stop=True)
+
+        for i in range(2):
+            nc.vector.tensor_copy(grouped[i][:, :, 3], window(3, i * Q, Q))
+        for r in range(2):
+            nc.scalar.activation(out=high_pair[:, 1, r * Q : (r + 1) * Q], in_=window(3, H + r * Q, Q), func=ACT.Copy)
+        for r in range(2):
+            nc.scalar.copy(out=grouped[2 + r][:, :, 2:4], in_=pair_view(high_pair, r))
+        for i in range(4):
+            score(i)
+
+        neg_all = keep.tile([P, 2, S], F32, name="neg_all", tag="high", align_bytes=64)
+        neg = [neg_all[:, m, :] for m in range(2)]
+        for i in range(2):
+            cols = slice(i * Q, (i + 1) * Q)
+            nc.vector.scalar_tensor_tensor(out=neg_all[:, :, cols], in0=early[i][:], scalar=-1.0, in1=prior_sb[:, cols].unsqueeze(1).to_broadcast([P, 2, Q]), op0=ALU.mult, op1=ALU.subtract)
+        for r in range(2):
+            cols = slice(H + r * Q, H + (r + 1) * Q)
+            nc.vector.scalar_tensor_tensor(out=neg[0][:, cols], in0=late0[r][:], scalar=-1.0, in1=prior_sb[:, cols], op0=ALU.mult, op1=ALU.subtract)
+        nc.vector.scalar_tensor_tensor(out=neg[1][:, H:S], in0=late1[:], scalar=-1.0, in1=prior_sb[:, H:S], op0=ALU.mult, op1=ALU.subtract)
+        low = [keep.tile([P, 1], F32, name="low%d" % m, tag=("prior", "low1")[m]) for m in range(2)]
         total = [keep.tile([P, 1], F32, name="total%d" % m) for m in range(2)]
         inv = [keep.tile([P, 1], F32, name="inv%d" % m) for m in range(2)]
         ex = [keep.tile([P, S], F32, name="ex%d" % m) for m in range(2)]

@@ -30,7 +30,7 @@ def tile_picked_rank_prior_e_kernel(tc, xT, w1_words, w1_scales, prior, offs, ou
         offsets = keep.tile([P, S // 16], U16, name="offsets")
         w_codes = keep.tile([P, N], U32, name="w_codes", align_bytes=64)
         w_scales = keep.tile([P, N], U8, name="w_scales", align_bytes=64)
-        prior_sb = keep.tile([P, S], F32, name="prior_sb", tag="prior")
+        prior_sb = keep.tile([P, S], F32, name="prior_sb")
         nc.vector.memset(w_scales[:].bitcast(I32), 0)
 
         warm_in = keep.tile([P, 1], F32, name="warm_in")
@@ -83,10 +83,12 @@ def tile_picked_rank_prior_e_kernel(tc, xT, w1_words, w1_scales, prior, offs, ou
             nc.vector.tensor_copy(grouped[i][:, :, 3], window(3, i * Q, Q))
         for r in range(2):
             nc.scalar.activation(out=high_pair[:, 1, r * Q : (r + 1) * Q], in_=window(3, H + r * Q, Q), func=ACT.Copy)
-        for r in range(2):
-            nc.scalar.copy(out=grouped[2 + r][:, :, 2:4], in_=pair_view(high_pair, r))
-        for i in range(4):
-            score(i)
+        nc.scalar.copy(out=grouped[3][:, :, 2:4], in_=pair_view(high_pair, 1))
+        score(0)
+        nc.vector.tensor_copy(out=grouped[2][:, :, 2:4], in_=pair_view(high_pair, 0))
+        score(1)
+        score(2)
+        score(3)
 
         neg_all = keep.tile([P, 2, S], F32, name="neg_all", tag="high", align_bytes=64)
         neg = [neg_all[:, m, :] for m in range(2)]
@@ -97,7 +99,7 @@ def tile_picked_rank_prior_e_kernel(tc, xT, w1_words, w1_scales, prior, offs, ou
             cols = slice(H + r * Q, H + (r + 1) * Q)
             nc.vector.scalar_tensor_tensor(out=neg[0][:, cols], in0=late0[r][:], scalar=-1.0, in1=prior_sb[:, cols], op0=ALU.mult, op1=ALU.subtract)
         nc.vector.scalar_tensor_tensor(out=neg[1][:, H:S], in0=late1[:], scalar=-1.0, in1=prior_sb[:, H:S], op0=ALU.mult, op1=ALU.subtract)
-        low = [keep.tile([P, 1], F32, name="low%d" % m, tag=("prior", "low1")[m]) for m in range(2)]
+        low = [keep.tile([P, 1], F32, name="low%d" % m) for m in range(2)]
         total = [keep.tile([P, 1], F32, name="total%d" % m) for m in range(2)]
         inv = [keep.tile([P, 1], F32, name="inv%d" % m) for m in range(2)]
         ex = [keep.tile([P, S], F32, name="ex%d" % m) for m in range(2)]
@@ -107,6 +109,10 @@ def tile_picked_rank_prior_e_kernel(tc, xT, w1_words, w1_scales, prior, offs, ou
             nc.scalar.activation(out=ex[m][:], in_=neg[m], func=ACT.Exp, bias=low[m][:], scale=-1.0, accum_out=total[m][:])
         for m in range(2):
             nc.vector.reciprocal(out=inv[m][:], in_=total[m][:])
-            for cols in ([slice(0, S)], [slice(0, H), slice(H, S)])[m]:
-                nc.vector.tensor_scalar(out=res[m][:, cols], in0=ex[m][:, cols], scalar1=inv[m][:], scalar2=None, op0=ALU.mult)
+            for half in range(2):
+                cols = slice(half * H, (half + 1) * H)
+                if (m, half) == (0, 1):
+                    nc.scalar.activation(out=res[m][:, cols], in_=ex[m][:, cols], func=ACT.Copy, scale=inv[m][:])
+                else:
+                    nc.vector.tensor_scalar(out=res[m][:, cols], in0=ex[m][:, cols], scalar1=inv[m][:], scalar2=None, op0=ALU.mult)
                 nc.sync.dma_start(out=out[m * P : (m + 1) * P, cols], in_=res[m][:, cols])

@@ -18,6 +18,7 @@ ACT = mybir.ActivationFunctionType
 
 Q = 128
 H = 256
+CUT = 64
 
 
 def tile_picked_rank_prior_e_kernel(tc, xT, w1_words, w1_scales, prior, offs, out):
@@ -83,9 +84,10 @@ def tile_picked_rank_prior_e_kernel(tc, xT, w1_words, w1_scales, prior, offs, ou
             nc.vector.tensor_copy(grouped[i][:, :, 3], window(3, i * Q, Q))
         for r in range(2):
             nc.scalar.activation(out=high_pair[:, 1, r * Q : (r + 1) * Q], in_=window(3, H + r * Q, Q), func=ACT.Copy)
+        nc.scalar.copy(out=grouped[2][:, CUT:Q, 2:4], in_=pair_view(high_pair, 0)[:, CUT:Q, :])
         nc.scalar.copy(out=grouped[3][:, :, 2:4], in_=pair_view(high_pair, 1))
         score(0)
-        nc.vector.tensor_copy(out=grouped[2][:, :, 2:4], in_=pair_view(high_pair, 0))
+        nc.vector.tensor_copy(out=grouped[2][:, 0:CUT, 2:4], in_=pair_view(high_pair, 0)[:, 0:CUT, :])
         score(1)
         score(2)
         score(3)

@@ -32,13 +32,13 @@ def tile_picked_rank_prior_e_kernel(tc, xT, w1_words, w1_scales, prior, offs, ou
         w_codes = keep.tile([P, N], U32, name="w_codes", align_bytes=64)
         w_scales = keep.tile([P, N], U8, name="w_scales", align_bytes=64)
         prior_sb = keep.tile([P, S], F32, name="prior_sb")
-        nc.vector.memset(w_scales[:].bitcast(I32), 0)
 
         warm_in = keep.tile([P, 1], F32, name="warm_in")
         warm_out = keep.tile([P, 1], F32, name="warm_out")
         nc.vector.memset(warm_in[:], 0.0)
         nc.scalar.activation(out=warm_out[:], in_=warm_in[:], func=ACT.Exp)
 
+        nc.vector.memset(w_scales[:].bitcast(I32), 0)
         planes = [keep.tile([P, T], F32, name="plane%d" % j, align_bytes=64) for j in range(4)]
         for j in range(4):
             nc.sync.dma_start(out=planes[j][:], in_=x4[:, j, :])
@@ -46,7 +46,7 @@ def tile_picked_rank_prior_e_kernel(tc, xT, w1_words, w1_scales, prior, offs, ou
                 nc.sync.dma_start(offsets[:], offs)
         nc.sync.dma_start(out=w_codes[:].bitcast(I32), in_=w1_words[0].rearrange("p n t -> p (n t)").bitcast(I32))
         for q in range(4):
-            nc.sync.dma_start(out=w_scales[32 * q : 32 * q + 4, :].bitcast(I32), in_=w1_scales[0, 4 * q : 4 * q + 4, :].bitcast(I32))
+            nc.scalar.dma_start(out=w_scales[32 * q : 32 * q + 4, :].bitcast(I32), in_=w1_scales[0, 4 * q : 4 * q + 4, :].bitcast(I32))
         nc.sync.dma_start(out=prior_sb[:], in_=prior)
 
         def window(j, first, count):

@@ -19,6 +19,8 @@ ACT = mybir.ActivationFunctionType
 Q = 128
 H = 256
 CUT = 64
+PITCH = Q + 1
+ROW1 = 4 * PITCH + 4
 
 
 def tile_picked_rank_prior_e_kernel(tc, xT, w1_words, w1_scales, prior, offs, out):
@@ -67,18 +69,23 @@ def tile_picked_rank_prior_e_kernel(tc, xT, w1_words, w1_scales, prior, offs, ou
                 for r in range(2):
                     nc.vector.tensor_copy(out=grouped[2 + r][:, :, 0:2], in_=pair_view(low_pair, r))
 
-        x_codes = [keep.tile([P, Q], U32, name="x_codes%d" % i, align_bytes=64) for i in range(4)]
-        x_scales = [keep.tile([P, Q], U8, name="x_scales%d" % i, align_bytes=64) for i in range(4)]
-        early = [psum.tile([P, 2, Q], F32, name="early%d" % i) for i in range(2)]
-        late0 = [psum.tile([P, Q], F32, name="late0_%d" % r) for r in range(2)]
+        half_codes = [keep.tile([P, H], U32, name="half_codes%d" % h, align_bytes=64) for h in range(2)]
+        half_scales = [keep.tile([P, H], U8, name="half_scales%d" % h, align_bytes=64) for h in range(2)]
+        x_codes = [half_codes[i // 2][:, (i % 2) * Q : (i % 2 + 1) * Q] for i in range(4)]
+        x_scales = [half_scales[i // 2][:, (i % 2) * Q : (i % 2 + 1) * Q] for i in range(4)]
+        bank0 = [psum.tile([P, Q], F32, name="bank0_%d" % i) for i in range(4)]
+        bank1 = [psum.tile([P, Q], F32, name="bank1_%d" % i) for i in range(2)]
         late1 = psum.tile([P, H], F32, name="late1")
 
+        def product(bank, m, codes, scales):
+            nc.tensor.matmul_mx(out=bank, lhsT=w_codes[:, m * P : (m + 1) * P].bitcast(FP8X4), lhsT_scale=w_scales[:, m * P : (m + 1) * P],
+                                rhs=codes.bitcast(FP8X4), rhs_scale=scales, start=True, stop=True)
+
         def score(i):
-            nc.vector.quantize_mx(out=x_codes[i][:].bitcast(FP8X4), scales=x_scales[i][:], in_=grouped[i][:].rearrange("p n t -> p (n t)"))
-            for m in range(2):
-                bank = early[i][:, m, :] if i < 2 else (late0[i - 2][:], late1[:, (i - 2) * Q : (i - 1) * Q])[m]
-                nc.tensor.matmul_mx(out=bank, lhsT=w_codes[:, m * P : (m + 1) * P].bitcast(FP8X4), lhsT_scale=w_scales[:, m * P : (m + 1) * P],
-                                    rhs=x_codes[i][:].bitcast(FP8X4), rhs_scale=x_scales[i][:], start=True, stop=True)
+            nc.vector.quantize_mx(out=x_codes[i].bitcast(FP8X4), scales=x_scales[i], in_=grouped[i][:].rearrange("p n t -> p (n t)"))
+            product(bank0[i][:], 0, x_codes[i], x_scales[i])
+            if i < 2:
+                product(bank1[i][:], 1, x_codes[i], x_scales[i])
 
         for i in range(2):
             nc.vector.tensor_copy(grouped[i][:, :, 3], window(3, i * Q, Q))
@@ -92,23 +99,39 @@ def tile_picked_rank_prior_e_kernel(tc, xT, w1_words, w1_scales, prior, offs, ou
         score(2)
         score(3)
 
-        neg_all = keep.tile([P, 2, S], F32, name="neg_all", tag="high", align_bytes=64)
-        neg = [neg_all[:, m, :] for m in range(2)]
-        for i in range(2):
-            cols = slice(i * Q, (i + 1) * Q)
-            nc.vector.scalar_tensor_tensor(out=neg_all[:, :, cols], in0=early[i][:], scalar=-1.0, in1=prior_sb[:, cols].unsqueeze(1).to_broadcast([P, 2, Q]), op0=ALU.mult, op1=ALU.subtract)
-        for r in range(2):
-            cols = slice(H + r * Q, H + (r + 1) * Q)
-            nc.vector.scalar_tensor_tensor(out=neg[0][:, cols], in0=late0[r][:], scalar=-1.0, in1=prior_sb[:, cols], op0=ALU.mult, op1=ALU.subtract)
-        nc.vector.scalar_tensor_tensor(out=neg[1][:, H:S], in0=late1[:], scalar=-1.0, in1=prior_sb[:, H:S], op0=ALU.mult, op1=ALU.subtract)
+        product(late1[:], 1, half_codes[1][:], half_scales[1][:])
+
+        neg_all = keep.tile([P, ROW1 + S], F32, name="neg_all", tag="high", align_bytes=64)
+        neg0 = [neg_all[:, i * PITCH : i * PITCH + Q] for i in range(4)]
+        neg1 = neg_all[:, ROW1 : ROW1 + S]
         low = [keep.tile([P, 1], F32, name="low%d" % m) for m in range(2)]
         total = [keep.tile([P, 1], F32, name="total%d" % m) for m in range(2)]
         inv = [keep.tile([P, 1], F32, name="inv%d" % m) for m in range(2)]
         ex = [keep.tile([P, S], F32, name="ex%d" % m) for m in range(2)]
         res = [keep.tile([P, S], F32, name="res%d" % m) for m in range(2)]
-        for m in range(2):
-            nc.vector.tensor_reduce(out=low[m][:], in_=neg[m], axis=mybir.AxisListType.X, op=ALU.min)
-            nc.scalar.activation(out=ex[m][:], in_=neg[m], func=ACT.Exp, bias=low[m][:], scale=-1.0, accum_out=total[m][:])
+        minus = [keep.tile([P, Q], F32, name="minus%d" % i) for i in range(2)]
+
+        def add_prior(dst, bank, first, count):
+            nc.vector.scalar_tensor_tensor(out=dst, in0=bank, scalar=-1.0, in1=prior_sb[:, first : first + count], op0=ALU.mult, op1=ALU.subtract)
+
+        def row_min(dst, values):
+            nc.vector.tensor_reduce(out=dst, in_=values, axis=mybir.AxisListType.X, op=ALU.min)
+
+        for i in range(2):
+            nc.scalar.activation(out=minus[i][:], in_=bank1[i][:], func=ACT.Copy, scale=-1.0)
+            nc.gpsimd.tensor_tensor(out=neg1[:, i * Q : (i + 1) * Q], in0=minus[i][:], in1=prior_sb[:, i * Q : (i + 1) * Q], op=ALU.subtract)
+        add_prior(neg0[0], bank0[0][:], 0, Q)
+        add_prior(neg0[1], bank0[1][:], Q, Q)
+        row_min(neg_all[:, 3 * PITCH - 1 : 3 * PITCH], neg0[0])
+        add_prior(neg0[2], bank0[2][:], 2 * Q, Q)
+        add_prior(neg0[3], bank0[3][:], 3 * Q, Q)
+        row_min(neg_all[:, 2 * PITCH - 1 : 2 * PITCH], neg0[1])
+        add_prior(neg1[:, H:S], late1[:], H, H)
+        row_min(low[0][:], neg_all[:, 2 * PITCH - 1 : 3 * PITCH + Q])
+        nc.scalar.activation(out=ex[0][:].rearrange("p (i n) -> p i n", i=4), in_=neg_all[:, 0 : 4 * PITCH].rearrange("p (i n) -> p i n", i=4)[:, :, 0:Q],
+                             func=ACT.Exp, bias=low[0][:], scale=-1.0, accum_out=total[0][:])
+        row_min(low[1][:], neg1)
+        nc.scalar.activation(out=ex[1][:], in_=neg1, func=ACT.Exp, bias=low[1][:], scale=-1.0, accum_out=total[1][:])
         for m in range(2):
             nc.vector.reciprocal(out=inv[m][:], in_=total[m][:])
             for half in range(2):

@@ -49,7 +49,8 @@ def tile_picked_rank_prior_e_kernel(tc, xT, w1_words, w1_scales, prior, offs, ou
         nc.sync.dma_start(out=w_codes[:].bitcast(I32), in_=w1_words[0].rearrange("p n t -> p (n t)").bitcast(I32))
         for q in range(4):
             nc.scalar.dma_start(out=w_scales[32 * q : 32 * q + 4, :].bitcast(I32), in_=w1_scales[0, 4 * q : 4 * q + 4, :].bitcast(I32))
-        nc.sync.dma_start(out=prior_sb[:], in_=prior)
+        for half in range(2):
+            nc.sync.dma_start(out=prior_sb[:, half * H : (half + 1) * H], in_=prior[:, half * H : (half + 1) * H])
 
         def window(j, first, count):
             return planes[j][:].indirect(offsets[:, first // 16 : (first + count) // 16])

@@ -135,10 +135,7 @@ def tile_picked_rank_prior_e_kernel(tc, xT, w1_words, w1_scales, prior, offs, ou
         nc.scalar.activation(out=ex[1][:], in_=neg1, func=ACT.Exp, bias=low[1][:], scale=-1.0, accum_out=total[1][:])
         for m in range(2):
             nc.vector.reciprocal(out=inv[m][:], in_=total[m][:])
-            for half in range(2):
-                cols = slice(half * H, (half + 1) * H)
-                if (m, half) == (0, 1):
-                    nc.scalar.activation(out=res[m][:, cols], in_=ex[m][:, cols], func=ACT.Copy, scale=inv[m][:])
-                else:
-                    nc.vector.tensor_scalar(out=res[m][:, cols], in0=ex[m][:, cols], scalar1=inv[m][:], scalar2=None, op0=ALU.mult)
+            cut = (Q, H)[m]
+            for cols in (slice(0, cut), slice(cut, S)):
+                nc.vector.tensor_scalar(out=res[m][:, cols], in0=ex[m][:, cols], scalar1=inv[m][:], scalar2=None, op0=ALU.mult)
                 nc.sync.dma_start(out=out[m * P : (m + 1) * P, cols], in_=res[m][:, cols])

from contextlib import ExitStack

import concourse.mybir as mybir

K, T, S, N = 512, 1024, 512, 256
P = 128
FLOPS = 2 * K * S * N

F32 = mybir.dt.float32
BF16 = mybir.dt.bfloat16
I32 = mybir.dt.int32
U32 = mybir.dt.uint32
U16 = mybir.dt.uint16
U8 = mybir.dt.uint8
FP8X4 = mybir.dt.float8_e4m3fn_x4
ALU = mybir.AluOpType
ACT = mybir.ActivationFunctionType

Q = 128
H = 256
CUT = 64
PITCH = Q + 1
ROW1 = 4 * PITCH + 4


def tile_picked_rank_prior_e_kernel(tc, xT, w1_words, w1_scales, prior, offs, out):
    nc = tc.nc
    x4 = xT.rearrange("(p j) t -> p j t", j=4)
    with ExitStack() as ctx:
        keep = ctx.enter_context(tc.tile_pool(name="keep", bufs=1))
        psum = ctx.enter_context(tc.psum_pool(name="psum", bufs=1))

        offsets = keep.tile([P, S // 16], U16, name="offsets")
        w_codes = keep.tile([P, N], U32, name="w_codes", align_bytes=64)
        w_scales = keep.tile([P, N], U8, name="w_scales", align_bytes=64)
        prior_sb = keep.tile([P, S], F32, name="prior_sb")

        warm_in = keep.tile([P, 1], F32, name="warm_in")
        warm_out = keep.tile([P, 1], F32, name="warm_out")
        nc.vector.memset(warm_in[:], 0.0)
        nc.scalar.activation(out=warm_out[:], in_=warm_in[:], func=ACT.Exp)

        nc.vector.memset(w_scales[:].bitcast(I32), 0)
        planes = [keep.tile([P, T], F32, name="plane%d" % j, align_bytes=64) for j in range(4)]
        for j in range(4):
            nc.sync.dma_start(out=planes[j][:], in_=x4[:, j, :])
            if j == 0:
                nc.sync.dma_start(offsets[:], offs)
        nc.sync.dma_start(out=w_codes[:].bitcast(I32), in_=w1_words[0].rearrange("p n t -> p (n t)").bitcast(I32))
        for q in range(4):
            nc.scalar.dma_start(out=w_scales[32 * q : 32 * q + 4, :].bitcast(I32), in_=w1_scales[0, 4 * q : 4 * q + 4, :].bitcast(I32))
        for half in range(2):
            nc.sync.dma_start(out=prior_sb[:, half * H : (half + 1) * H], in_=prior[:, half * H : (half + 1) * H])

        def window(j, first, count):
            return planes[j][:].indirect(offsets[:, first // 16 : (first + count) // 16])

        grouped = [keep.tile([P, Q, 4], BF16, name="grouped%d" % i, align_bytes=64) for i in range(4)]
        low_pair = keep.tile([P, 2, H], BF16, name="low_pair", align_bytes=64)
        high_pair = keep.tile([P, 2, H], BF16, name="high_pair", tag="high", align_bytes=64)

        def pair_view(pair, r):
            return pair[:, :, r * Q : (r + 1) * Q].rearrange("p e n -> p n e")

        for j in range(3):
            for i in range(2):
                nc.vector.tensor_copy(grouped[i][:, :, j], window(j, i * Q, Q))
            nc.scalar.activation(out=(low_pair, high_pair)[j // 2][:, j % 2, :], in_=window(j, H, H), func=ACT.Copy)
            if j == 1:
                for r in range(2):
                    nc.vector.tensor_copy(out=grouped[2 + r][:, :, 0:2], in_=pair_view(low_pair, r))

        half_codes = [keep.tile([P, H], U32, name="half_codes%d" % h, align_bytes=64) for h in range(2)]
        half_scales = [keep.tile([P, H], U8, name="half_scales%d" % h, align_bytes=64) for h in range(2)]
        x_codes = [half_codes[i // 2][:, (i % 2) * Q : (i % 2 + 1) * Q] for i in range(4)]
        x_scales = [half_scales[i // 2][:, (i % 2) * Q : (i % 2 + 1) * Q] for i in range(4)]
        bank0 = [psum.tile([P, Q], F32, name="bank0_%d" % i) for i in range(4)]
        bank1 = [psum.tile([P, Q], F32, name="bank1_%d" % i) for i in range(2)]
        late1 = psum.tile([P, H], F32, name="late1")

        def product(bank, m, codes, scales):
            nc.tensor.matmul_mx(out=bank, lhsT=w_codes[:, m * P : (m + 1) * P].bitcast(FP8X4), lhsT_scale=w_scales[:, m * P : (m + 1) * P],
                                rhs=codes.bitcast(FP8X4), rhs_scale=scales, start=True, stop=True)

        def score(i):
            nc.vector.quantize_mx(out=x_codes[i].bitcast(FP8X4), scales=x_scales[i], in_=grouped[i][:].rearrange("p n t -> p (n t)"))
            product(bank0[i][:], 0, x_codes[i], x_scales[i])
            if i < 2:
                product(bank1[i][:], 1, x_codes[i], x_scales[i])

        for i in range(2):
            nc.vector.tensor_copy(grouped[i][:, :, 3], window(3, i * Q, Q))
        for r in range(2):
            nc.scalar.activation(out=high_pair[:, 1, r * Q : (r + 1) * Q], in_=window(3, H + r * Q, Q), func=ACT.Copy)
        nc.scalar.copy(out=grouped[2][:, CUT:Q, 2:4], in_=pair_view(high_pair, 0)[:, CUT:Q, :])
        nc.scalar.copy(out=grouped[3][:, :, 2:4], in_=pair_view(high_pair, 1))
        score(0)
        nc.vector.tensor_copy(out=grouped[2][:, 0:CUT, 2:4], in_=pair_view(high_pair, 0)[:, 0:CUT, :])
        score(1)
        score(2)
        score(3)

        product(late1[:], 1, half_codes[1][:], half_scales[1][:])

        neg_all = keep.tile([P, ROW1 + S], F32, name="neg_all", tag="high", align_bytes=64)
        neg0 = [neg_all[:, i * PITCH : i * PITCH + Q] for i in range(4)]
        neg1 = neg_all[:, ROW1 : ROW1 + S]
        low = [keep.tile([P, 1], F32, name="low%d" % m) for m in range(2)]
        total = [keep.tile([P, 1], F32, name="total%d" % m) for m in range(2)]
        inv = [keep.tile([P, 1], F32, name="inv%d" % m) for m in range(2)]
        ex = [keep.tile([P, S], F32, name="ex%d" % m) for m in range(2)]
        res = [keep.tile([P, S], F32, name="res%d" % m) for m in range(2)]
        minus = [keep.tile([P, Q], F32, name="minus%d" % i) for i in range(2)]

        def add_prior(dst, bank, first, count):
            nc.vector.scalar_tensor_tensor(out=dst, in0=bank, scalar=-1.0, in1=prior_sb[:, first : first + count], op0=ALU.mult, op1=ALU.subtract)

        def row_min(dst, values):
            nc.vector.tensor_reduce(out=dst, in_=values, axis=mybir.AxisListType.X, op=ALU.min)

        for i in range(2):
            nc.scalar.activation(out=minus[i][:], in_=bank1[i][:], func=ACT.Copy, scale=-1.0)
            nc.gpsimd.tensor_tensor(out=neg1[:, i * Q : (i + 1) * Q], in0=minus[i][:], in1=prior_sb[:, i * Q : (i + 1) * Q], op=ALU.subtract)
        add_prior(neg0[0], bank0[0][:], 0, Q)
        add_prior(neg0[1], bank0[1][:], Q, Q)
        row_min(neg_all[:, 3 * PITCH - 1 : 3 * PITCH], neg0[0])
        add_prior(neg0[2], bank0[2][:], 2 * Q, Q)
        add_prior(neg0[3], bank0[3][:], 3 * Q, Q)
        row_min(neg_all[:, 2 * PITCH - 1 : 2 * PITCH], neg0[1])
        add_prior(neg1[:, H:S], late1[:], H, H)
        row_min(low[0][:], neg_all[:, 2 * PITCH - 1 : 3 * PITCH + Q])
        nc.scalar.activation(out=ex[0][:].rearrange("p (i n) -> p i n", i=4), in_=neg_all[:, 0 : 4 * PITCH].rearrange("p (i n) -> p i n", i=4)[:, :, 0:Q],
                             func=ACT.Exp, bias=low[0][:], scale=-1.0, accum_out=total[0][:])
        row_min(low[1][:], neg1)
        nc.scalar.activation(out=ex[1][:], in_=neg1, func=ACT.Exp, bias=low[1][:], scale=-1.0, accum_out=total[1][:])
        for m in range(2):
            nc.vector.reciprocal(out=inv[m][:], in_=total[m][:])
            cut = (Q, H)[m]
            for cols in (slice(0, cut), slice(cut, S)):
                nc.vector.tensor_scalar(out=res[m][:, cols], in0=ex[m][:, cols], scalar1=inv[m][:], scalar2=None, op0=ALU.mult)
                nc.sync.dma_start(out=out[m * P : (m + 1) * P, cols], in_=res[m][:, cols])
